import numpy as np
import ml_dtypes


def mxq(x, axis, fmt="e4m3"):
    dtype, down = {"e4m3": (ml_dtypes.float8_e4m3fn, 7), "e5m2": (ml_dtypes.float8_e5m2, 14)}[fmt]
    v = np.moveaxis(np.asarray(x, np.float32).astype(ml_dtypes.bfloat16).astype(np.float64), axis, -1)
    blocks = v.reshape(v.shape[:-1] + (-1, 32))
    amax = np.abs(blocks).max(-1, keepdims=True)
    byte = np.maximum(np.where(amax > 0, np.frexp(amax)[1] - 1 + 127, 0) - down, 1)
    scale = np.exp2(byte - 127.0)
    codes = (blocks / scale).astype(np.float32).astype(dtype).astype(np.float64)
    return np.moveaxis((codes * scale).reshape(v.shape), -1, axis)


WIDE = False


def mx_kscale(k):
    if not WIDE:
        return np.ones(k)
    levels = np.array([10, -10, 5, -5, 0])
    if k % 512:
        return np.exp2(np.random.permutation(np.resize(levels, k // 32))).repeat(32)
    a = np.empty((k // 512, 16))
    for p in range(k // 512):
        a[p, :8] = np.random.permutation(np.resize(levels, 8))
        for g in range(8):
            far = levels[np.abs(levels - a[p, g]) >= 10]
            a[p, g + 8] = far[np.random.randint(len(far))]
    return np.exp2(a.ravel()).repeat(32)


def f64(x):
    return np.asarray(x).astype(np.float64)


def striped(idx):
    return np.tile(idx.reshape(-1, 16).T, (8, 1)).astype(np.uint16)


def unstriped(offs):
    return offs[:16].T.reshape(-1).astype(np.int64)


def striped8(idx):
    return np.concatenate([x.reshape(-1, 16).T for x in idx]).astype(np.uint16)


def runs(offs, k):
    lists = np.stack([offs[16 * r : 16 * r + 16].T.reshape(-1) for r in range(8)]).astype(np.int64)
    return lists[np.arange(k) % 512 // 64]


def pack_weight(w):
    k, n = w.shape
    w = f64(np.asarray(w, np.float32).astype(ml_dtypes.bfloat16)).reshape(k // 32, 32, n)
    amax = np.abs(w).max(1)
    byte = np.clip(np.where(amax > 0, np.frexp(amax)[1] - 1 + 127 - 7, 1), 1, 254)
    scaled = (w * np.exp2(127.0 - byte)[:, None, :]).reshape(k, n).astype(np.float32)
    words = np.ascontiguousarray(scaled.reshape(k // 512, 128, 4, n).transpose(0, 1, 3, 2)).astype(ml_dtypes.float8_e4m3fn).view(np.uint8)
    return words, np.ascontiguousarray(byte.astype(np.uint8).reshape(k // 512, 16, n))


def unpack_weight(words, scales):
    g, p, n, _ = words.shape
    vals = np.ascontiguousarray(words).view(ml_dtypes.float8_e4m3fn).astype(np.float64) * np.repeat(np.exp2(scales.astype(np.float64) - 127.0), 8, axis=1)[..., None]
    return vals.transpose(0, 1, 3, 2).reshape(g * 512, n)


def relu(v):
    return np.maximum(v, 0.0)


K, T, S, G, H, J, W = 512, 2048, 512, 2048, 512, 512, 384


def setup_inputs():
    n = np.random.standard_normal
    s = mx_kscale(K)[:, None]
    u = mx_kscale(S)
    packed_xT = pack_weight(n((K, T)) * s)
    packed_dT = pack_weight(n((K, G)) / s)
    return {
        "x_words": packed_xT[0],
        "x_scales": packed_xT[1],
        "d_words": packed_dT[0],
        "d_scales": packed_dT[1],
        "tab": n((H, J)).astype(np.float32),
        "ga": (np.random.uniform(0.5, 1.5, (H, 1)) * u[:, None]).astype(np.float32),
        "gb": (np.random.uniform(0.5, 1.5, (H, 1)) / u[:, None]).astype(np.float32),
        "offs": striped(np.random.permutation(T)[:S]),
        "kidx": striped8(np.random.randint(0, G, (8, H))),
        "n1": striped8(np.stack([np.random.permutation(S) for _ in range(8)])),
        "n2": striped8(np.random.randint(0, J, (8, S))),
        "n3": striped8(np.stack([np.random.permutation(S) for _ in range(8)])),
        "n4": striped(np.random.permutation(S)[:W]),
        "n5": striped(np.random.permutation(S)[:W]),
    }


def reference(x_words, x_scales, d_words, d_scales, tab, ga, gb, offs, kidx, n1, n2, n3, n4, n5):
    d_kidx = unpack_weight(d_words, d_scales)[np.arange(K)[:, None], runs(kidx, K)]
    xq = unpack_weight(x_words, x_scales)[:, unstriped(offs)]
    s = 0.0625 * (d_kidx.T @ xq)
    rl = relu(s)
    ds = np.zeros((H, S))
    ds[np.arange(H)[:, None], runs(n1, H)] = rl
    z = f64(ga) * (ds - (0.5 * s))
    z2 = f64(gb) * (np.maximum(s + f64(tab)[np.arange(H)[:, None], runs(n2, H)], s[np.arange(H)[:, None], runs(n3, H)]))
    cm = 0.0625 * ((mxq(z, 0, "e4m3").T @ mxq(z2, 0, "e4m3")))
    old = cm[:, unstriped(n4)]
    pa = cm[:, unstriped(n5)]
    ra = old - (0.5 * pa)
    out = cm.copy()
    out[:, unstriped(n4)] = ra
    return out

@@ -1,0 +1,206 @@
+from contextlib import ExitStack
+
+import concourse.mybir as mybir
+
+K, T, S, W = 512, 2048, 512, 384
+FLOPS = 2 * 2 * K * S * S
+
+F32 = mybir.dt.float32
+BF16 = mybir.dt.bfloat16
+I32 = mybir.dt.int32
+U32 = mybir.dt.uint32
+U16 = mybir.dt.uint16
+U8 = mybir.dt.uint8
+FP8X4 = mybir.dt.float8_e4m3fn_x4
+ALU = mybir.AluOpType
+ACT = mybir.ActivationFunctionType
+
+P = 128
+PACK = 4
+SIXTEENTH = 0.0625
+
+
+def tile_picked_simksendkindkdif_none_p_kernel(
+    tc, x_words, x_scales, d_words, d_scales, tab, ga, gb, offs, kidx, n1, n2, n3, n4, n5, out
+):
+    nc = tc.nc
+    with ExitStack() as ctx:
+        lists = ctx.enter_context(tc.tile_pool(name="lists", bufs=1))
+        keep = ctx.enter_context(tc.tile_pool(name="keep", bufs=1))
+        psum = ctx.enter_context(tc.psum_pool(name="psum", bufs=1))
+
+        def load_list(name, src):
+            tile = lists.tile(list(src.shape), U16, name=name)
+            nc.sync.dma_start(tile[:], src)
+            return tile
+
+        d_scale_table = keep.tile([P, T], U8, name="d_scale_table", tag="table0")
+        x_scale_table = keep.tile([P, T], U8, name="x_scale_table", tag="table1")
+        planes = keep.tile([P, 2 * S], U8, name="planes", align_bytes=64)
+        nc.gpsimd.memset(d_scale_table[:].bitcast(I32), 0)
+        nc.vector.memset(x_scale_table[:].bitcast(I32), 0)
+        nc.gpsimd.memset(planes[:].bitcast(I32), 0)
+        nc.scalar.dma_start(d_scale_table[0:P:8, :].bitcast(I32), d_scales[0].bitcast(I32))
+        nc.scalar.dma_start(x_scale_table[0:P:8, :].bitcast(I32), x_scales[0].bitcast(I32))
+
+        kidx_t = load_list("kidx_t", kidx)
+        offs_t = load_list("offs_t", offs)
+        ga_t = keep.tile([P, PACK], F32, name="ga_t")
+        gb_t = keep.tile([P, PACK], F32, name="gb_t")
+        nc.sync.dma_start(gb_t[:], gb.rearrange("(p t) o -> p (t o)", t=PACK))
+        nc.sync.dma_start(ga_t[:], ga.rearrange("(p t) o -> p (t o)", t=PACK))
+        n2_t = load_list("n2_t", n2)
+        d_word_table = keep.tile([P, T], I32, name="d_word_table", tag="table2")
+        nc.sync.dma_start(d_word_table[:], d_words[0].rearrange("p n t -> p (n t)").bitcast(I32))
+        x_word_table = keep.tile([P, T], I32, name="x_word_table", tag="table3")
+        nc.sync.dma_start(x_word_table[:], x_words[0].rearrange("p n t -> p (n t)").bitcast(I32))
+        n1_t = load_list("n1_t", n1)
+        n3_t = load_list("n3_t", n3)
+        n4_t = load_list("n4_t", n4)
+        n5_t = load_list("n5_t", n5)
+
+        sign = keep.tile([P, PACK], F32, name="sign")
+        twice = keep.tile([P, PACK], F32, name="twice")
+        gb_abs = keep.tile([P, PACK], F32, name="gb_abs")
+        gb_score = keep.tile([P, PACK], F32, name="gb_score")
+        ga_signed = keep.tile([P, PACK], F32, name="ga_signed")
+        ga_score = keep.tile([P, PACK], F32, name="ga_score")
+        nc.gpsimd.tensor_scalar(twice[:], gb_t[:], 0.0, 2.0, ALU.is_ge, ALU.mult)
+        nc.gpsimd.tensor_scalar(sign[:], twice[:], 1.0, -1.0, ALU.mult, ALU.add)
+        nc.gpsimd.tensor_tensor(ga_signed[:], ga_t[:], sign[:], ALU.mult)
+        nc.scalar.activation(gb_abs[:], gb_t[:], ACT.Abs)
+        nc.scalar.activation(gb_score[:], gb_t[:], ACT.Abs, scale=SIXTEENTH)
+        nc.gpsimd.tensor_scalar(ga_score[:], ga_signed[:], -0.5 * SIXTEENTH, 0.0, ALU.mult, ALU.add)
+        ga_rows = keep.tile([P, PACK, S], F32, name="ga_rows")
+        nc.scalar.activation(ga_rows[:], ga_signed[:].unsqueeze(2).to_broadcast([P, PACK, S]), ACT.Copy)
+        minus_half = keep.tile([P, W], F32, name="minus_half")
+        nc.gpsimd.memset(minus_half[:], -0.5)
+
+        d_bytes = keep.tile([P, S], U8, name="d_bytes")
+        nc.vector.tensor_copy(d_bytes[:], d_scale_table[:].indirect(kidx_t[:]))
+        staged = keep.tile([P, 2 * S], U8, name="staged")
+        nc.vector.tensor_copy(
+            staged[:, :S].rearrange("p (t m) -> p t m", t=PACK), d_bytes[:].rearrange("p (m t) -> p t m", t=PACK)
+        )
+        x_bytes = keep.tile([P, S], U8, name="x_bytes")
+        nc.vector.tensor_copy(x_bytes[:], x_scale_table[:].indirect(offs_t[:]))
+        nc.vector.tensor_copy(staged[:, S:].bitcast(I32), x_bytes[:].bitcast(I32))
+        for q in range(4):
+            nc.scalar.dma_start(planes[32 * q : 32 * q + 4, :].bitcast(I32), staged[32 * q : 32 * q + 32 : 8, :].bitcast(I32))
+
+        d_picked = keep.tile([P, S], U32, name="d_picked")
+        nc.vector.tensor_copy(d_picked[:], d_word_table[:].bitcast(U32).indirect(kidx_t[:]))
+        d_codes = keep.tile([P, S], U32, name="d_codes", align_bytes=64)
+        nc.vector.tensor_copy(
+            d_codes[:].bitcast(I32).rearrange("p (t c i) -> p c t i", t=PACK, i=4),
+            d_picked[:].bitcast(I32).rearrange("p (c i t) -> p c t i", t=PACK, i=4),
+        )
+        x_codes = keep.tile([P, S], U32, name="x_codes", align_bytes=64)
+        nc.vector.tensor_copy(x_codes[:], x_word_table[:].bitcast(U32).indirect(offs_t[:]))
+
+        tab_rows = tab.rearrange("(p t) j -> t p j", t=PACK)
+        tab_t = []
+        for t in range(PACK):
+            tile = keep.tile([P, S], F32, name=f"tab{t}", tag=f"table{t}")
+            nc.sync.dma_start(tile[:], tab_rows[t])
+            tab_t.append(tile)
+
+        score_bank = []
+        for t in range(PACK):
+            bank = psum.tile([P, S], F32, name=f"score_bank{t}")
+            cols = slice(P * t, P * t + P)
+            nc.tensor.matmul_mx(
+                out=bank[:], lhsT=d_codes[:, cols].bitcast(FP8X4), lhsT_scale=planes[:, cols],
+                rhs=x_codes[:].bitcast(FP8X4), rhs_scale=planes[:, S:], start=True, stop=True,
+            )
+            score_bank.append(bank)
+
+        z_rows = keep.tile([P, PACK, S], BF16, name="z_rows")
+        z2_rows = keep.tile([P, PACK, S], BF16, name="z2_rows")
+        scores, sent = [], []
+        for t in range(PACK):
+            both = keep.tile([P, 2 * S], F32, name=f"scores{t}")
+            nc.scalar.activation(both[:, S:], score_bank[t][:], ACT.Relu, scale=SIXTEENTH)
+            nc.scalar.activation(both[:, :S], score_bank[t][:], ACT.Copy, scale=gb_score[:, t : t + 1])
+            scores.append(both)
+            sent.append(keep.tile([P, 2 * S], F32, name=f"sent{t}"))
+
+        half = S // 2
+        tab_picked = keep.tile([P, PACK, S], F32, name="tab_picked")
+        for t in range(PACK):
+            for h in range(2):
+                nc.scalar.activation(
+                    tab_picked[:, t, h * half : (h + 1) * half], tab_t[t][:].indirect(n2_t[:, 16 * h : 16 * h + 16]), ACT.Copy
+                )
+
+        def send(t):
+            nc.vector.tensor_tensor(sent[t][:].indirect(n1_t[:]), scores[t][:, S:], ga_rows[:, t, :], ALU.mult)
+
+        def make_z(t):
+            nc.vector.scalar_tensor_tensor(z_rows[:, t, :], score_bank[t][:], ga_score[:, t : t + 1], sent[t][:, :S], ALU.mult, ALU.add)
+
+        def make_z2(t):
+            fetched = keep.tile([P, S], F32, name=f"fetched{t}")
+            nc.scalar.activation(fetched[:], scores[t][:].indirect(n3_t[:]), ACT.Copy)
+            summed = keep.tile([P, S], F32, name=f"summed{t}")
+            nc.vector.scalar_tensor_tensor(summed[:], tab_picked[:, t, :], gb_abs[:, t : t + 1], scores[t][:, :S], ALU.mult, ALU.add)
+            nc.vector.tensor_tensor(z2_rows[:, t, :], summed[:], fetched[:], ALU.max)
+
+        def interleave(copy, grouped, rows, cols):
+            copy(
+                grouped[:, cols, :].rearrange("p (c i) t -> p c t i", i=4),
+                rows[:, :, cols].rearrange("p t (c i) -> p c t i", i=4),
+            )
+
+        send(0)
+        send(1)
+        make_z2(0)
+        make_z2(1)
+        make_z(0)
+        send(2)
+        make_z2(2)
+        make_z2(3)
+        make_z(1)
+        z2_grouped = keep.tile([P, S, PACK], BF16, name="z2_grouped", align_bytes=64)
+        interleave(nc.scalar.copy, z2_grouped, z2_rows, slice(0, S))
+        send(3)
+        make_z(2)
+        make_z(3)
+        z2_codes = keep.tile([P, S], U32, name="z2_codes", align_bytes=64)
+        z2_plane = keep.tile([P, S], U8, name="z2_plane", align_bytes=64)
+        nc.vector.quantize_mx(out=z2_codes[:].bitcast(FP8X4), scales=z2_plane[:], in_=z2_grouped[:].rearrange("p c t -> p (c t)"))
+
+        z_grouped = keep.tile([P, S, PACK], BF16, name="z_grouped", align_bytes=64)
+        z_codes = keep.tile([P, S], U32, name="z_codes", align_bytes=64)
+        z_plane = keep.tile([P, S], U8, name="z_plane", align_bytes=64)
+        cm_bank = []
+        for b in range(S // P):
+            cols = slice(P * b, P * b + P)
+            interleave(nc.scalar.copy if b % 2 else nc.vector.tensor_copy, z_grouped, z_rows, cols)
+        for b in range(S // P):
+            cols = slice(P * b, P * b + P)
+            nc.vector.quantize_mx(out=z_codes[:, cols].bitcast(FP8X4), scales=z_plane[:, cols], in_=z_grouped[:, cols, :].rearrange("p c t -> p (c t)"))
+            bank = psum.tile([P, S], F32, name=f"cm_bank{b}")
+            nc.tensor.matmul_mx(
+                out=bank[:], lhsT=z_codes[:, cols].bitcast(FP8X4), lhsT_scale=z_plane[:, cols],
+                rhs=z2_codes[:].bitcast(FP8X4), rhs_scale=z2_plane[:], start=True, stop=True,
+            )
+            cm_bank.append(bank)
+
+        for b in range(S // P):
+            cm = keep.tile([P, S], F32, name=f"cm{b}")
+            pulled = keep.tile([P, W], F32, name=f"pulled{b}")
+            second = keep.tile([P, W], F32, name=f"second{b}")
+            if b % 2 == 0:
+                nc.scalar.activation(cm[:], cm_bank[b][:], ACT.Copy, scale=SIXTEENTH)
+                nc.scalar.activation(pulled[:], cm[:].indirect(n5_t[:]), ACT.Copy, scale=-0.5)
+                nc.scalar.activation(second[:], cm[:].indirect(n4_t[:]), ACT.Copy)
+                for h in range(2):
+                    cols = slice(h * W // 2, (h + 1) * W // 2)
+                    nc.vector.tensor_tensor(cm[:].indirect(n4_t[:, 12 * h : 12 * h + 12]), second[:, cols], pulled[:, cols], ALU.add)
+            else:
+                nc.vector.tensor_scalar(cm[:], cm_bank[b][:], SIXTEENTH, None, ALU.mult)
+                nc.vector.tensor_tensor(pulled[:], cm[:].indirect(n5_t[:]), minus_half[:], ALU.mult)
+                nc.vector.tensor_tensor(second[:], cm[:].indirect(n4_t[:]), pulled[:], ALU.add)
+                nc.scalar.activation(cm[:].indirect(n4_t[:]), second[:], ACT.Copy)
+            nc.sync.dma_start(out[P * b : P * b + P, :], cm[:])

@@ -34,51 +34,47 @@ def tile_picked_simksendkindkdif_none_p_kernel(
             nc.sync.dma_start(tile[:], src)
             return tile
 
-        d_scale_table = keep.tile([P, T], U8, name="d_scale_table", tag="table0")
-        x_scale_table = keep.tile([P, T], U8, name="x_scale_table", tag="table1")
+        d_scale_table = keep.tile([P, T], U8, name="d_scale_table")
+        x_scale_table = keep.tile([P, T], U8, name="x_scale_table")
         planes = keep.tile([P, 2 * S], U8, name="planes", align_bytes=64)
-        nc.gpsimd.memset(d_scale_table[:].bitcast(I32), 0)
-        nc.vector.memset(x_scale_table[:].bitcast(I32), 0)
         nc.gpsimd.memset(planes[:].bitcast(I32), 0)
-        nc.scalar.dma_start(d_scale_table[0:P:8, :].bitcast(I32), d_scales[0].bitcast(I32))
-        nc.scalar.dma_start(x_scale_table[0:P:8, :].bitcast(I32), x_scales[0].bitcast(I32))
 
-        kidx_t = load_list("kidx_t", kidx)
-        offs_t = load_list("offs_t", offs)
         ga_t = keep.tile([P, PACK], F32, name="ga_t")
         gb_t = keep.tile([P, PACK], F32, name="gb_t")
-        nc.sync.dma_start(gb_t[:], gb.rearrange("(p t) o -> p (t o)", t=PACK))
-        nc.sync.dma_start(ga_t[:], ga.rearrange("(p t) o -> p (t o)", t=PACK))
-        n2_t = load_list("n2_t", n2)
-        d_word_table = keep.tile([P, T], I32, name="d_word_table", tag="table2")
+        kidx_t = load_list("kidx_t", kidx)
+        nc.scalar.dma_start(gb_t[:], gb.rearrange("(p t) o -> p (t o)", t=PACK))
+        nc.scalar.dma_start(ga_t[:], ga.rearrange("(p t) o -> p (t o)", t=PACK))
+        nc.sync.dma_start(d_scale_table[:].bitcast(I32), d_scales[0].bitcast(I32).unsqueeze(1).to_broadcast([16, 8, T // 4]))
+        offs_t = load_list("offs_t", offs)
+        nc.sync.dma_start(x_scale_table[:].bitcast(I32), x_scales[0].bitcast(I32).unsqueeze(1).to_broadcast([16, 8, T // 4]))
+        d_word_table = keep.tile([P, T], I32, name="d_word_table", tag="table0")
         nc.sync.dma_start(d_word_table[:], d_words[0].rearrange("p n t -> p (n t)").bitcast(I32))
-        x_word_table = keep.tile([P, T], I32, name="x_word_table", tag="table3")
+        x_word_table = keep.tile([P, T], I32, name="x_word_table", tag="table2")
         nc.sync.dma_start(x_word_table[:], x_words[0].rearrange("p n t -> p (n t)").bitcast(I32))
+        n2_t = load_list("n2_t", n2)
         n1_t = load_list("n1_t", n1)
         n3_t = load_list("n3_t", n3)
         n4_t = load_list("n4_t", n4)
         n5_t = load_list("n5_t", n5)
 
-        sign = keep.tile([P, PACK], F32, name="sign")
-        twice = keep.tile([P, PACK], F32, name="twice")
+        half_sign = keep.tile([P, PACK], F32, name="half_sign")
         gb_abs = keep.tile([P, PACK], F32, name="gb_abs")
         gb_score = keep.tile([P, PACK], F32, name="gb_score")
-        ga_signed = keep.tile([P, PACK], F32, name="ga_signed")
+        ga_half = keep.tile([P, PACK], F32, name="ga_half")
         ga_score = keep.tile([P, PACK], F32, name="ga_score")
-        nc.gpsimd.tensor_scalar(twice[:], gb_t[:], 0.0, 2.0, ALU.is_ge, ALU.mult)
-        nc.gpsimd.tensor_scalar(sign[:], twice[:], 1.0, -1.0, ALU.mult, ALU.add)
-        nc.gpsimd.tensor_tensor(ga_signed[:], ga_t[:], sign[:], ALU.mult)
+        nc.gpsimd.tensor_scalar(half_sign[:], gb_t[:], 0.0, 0.5, ALU.is_ge, ALU.subtract)
+        nc.gpsimd.tensor_tensor(ga_half[:], ga_t[:], half_sign[:], ALU.mult)
+        nc.gpsimd.tensor_scalar(ga_score[:], ga_half[:], -SIXTEENTH, 0.0, ALU.mult, ALU.add)
         nc.scalar.activation(gb_abs[:], gb_t[:], ACT.Abs)
         nc.scalar.activation(gb_score[:], gb_t[:], ACT.Abs, scale=SIXTEENTH)
-        nc.gpsimd.tensor_scalar(ga_score[:], ga_signed[:], -0.5 * SIXTEENTH, 0.0, ALU.mult, ALU.add)
         ga_rows = keep.tile([P, PACK, S], F32, name="ga_rows")
-        nc.scalar.activation(ga_rows[:], ga_signed[:].unsqueeze(2).to_broadcast([P, PACK, S]), ACT.Copy)
+        nc.scalar.activation(ga_rows[:], ga_half[:].unsqueeze(2).to_broadcast([P, PACK, S]), ACT.Copy, scale=2.0)
         minus_half = keep.tile([P, W], F32, name="minus_half")
         nc.gpsimd.memset(minus_half[:], -0.5)
 
         d_bytes = keep.tile([P, S], U8, name="d_bytes")
         nc.vector.tensor_copy(d_bytes[:], d_scale_table[:].indirect(kidx_t[:]))
-        staged = keep.tile([P, 2 * S], U8, name="staged")
+        staged = keep.tile([P, 2 * S], U8, name="staged", tag="table3")
         nc.vector.tensor_copy(
             staged[:, :S].rearrange("p (t m) -> p t m", t=PACK), d_bytes[:].rearrange("p (m t) -> p t m", t=PACK)
         )
@@ -88,7 +84,7 @@ def tile_picked_simksendkindkdif_none_p_kernel(
         for q in range(4):
             nc.scalar.dma_start(planes[32 * q : 32 * q + 4, :].bitcast(I32), staged[32 * q : 32 * q + 32 : 8, :].bitcast(I32))
 
-        d_picked = keep.tile([P, S], U32, name="d_picked")
+        d_picked = keep.tile([P, S], U32, name="d_picked", tag="table1")
         nc.vector.tensor_copy(d_picked[:], d_word_table[:].bitcast(U32).indirect(kidx_t[:]))
         d_codes = keep.tile([P, S], U32, name="d_codes", align_bytes=64)
         nc.vector.tensor_copy(
@@ -96,7 +92,11 @@ def tile_picked_simksendkindkdif_none_p_kernel(
             d_picked[:].bitcast(I32).rearrange("p (c i t) -> p c t i", t=PACK, i=4),
         )
         x_codes = keep.tile([P, S], U32, name="x_codes", align_bytes=64)
-        nc.vector.tensor_copy(x_codes[:], x_word_table[:].bitcast(U32).indirect(offs_t[:]))
+        half = S // 2
+        halves = [slice(0, half), slice(half, S)]
+        list_halves = [slice(0, half // 16), slice(half // 16, S // 16)]
+        for h in range(2):
+            nc.vector.tensor_copy(x_codes[:, halves[h]], x_word_table[:].bitcast(U32).indirect(offs_t[:, list_halves[h]]))
 
         tab_rows = tab.rearrange("(p t) j -> t p j", t=PACK)
         tab_t = []
@@ -105,46 +105,54 @@ def tile_picked_simksendkindkdif_none_p_kernel(
             nc.sync.dma_start(tile[:], tab_rows[t])
             tab_t.append(tile)
 
+        pieces = [(0, halves[0], list_halves[0]), (0, halves[1], list_halves[1])]
+        pieces = pieces + [(t, slice(0, S), slice(0, S // 16)) for t in range(1, PACK)]
         score_bank = []
-        for t in range(PACK):
-            bank = psum.tile([P, S], F32, name=f"score_bank{t}")
-            cols = slice(P * t, P * t + P)
+        for n, (t, cols, entries) in enumerate(pieces):
+            bank = psum.tile([P, cols.stop - cols.start], F32, name=f"score_bank{n}", tag=f"bank{n}")
+            keys = slice(P * t, P * t + P)
             nc.tensor.matmul_mx(
-                out=bank[:], lhsT=d_codes[:, cols].bitcast(FP8X4), lhsT_scale=planes[:, cols],
-                rhs=x_codes[:].bitcast(FP8X4), rhs_scale=planes[:, S:], start=True, stop=True,
+                out=bank[:], lhsT=d_codes[:, keys].bitcast(FP8X4), lhsT_scale=planes[:, keys],
+                rhs=x_codes[:, cols].bitcast(FP8X4), rhs_scale=planes[:, S + cols.start : S + cols.stop], start=True, stop=True,
             )
             score_bank.append(bank)
 
         z_rows = keep.tile([P, PACK, S], BF16, name="z_rows")
         z2_rows = keep.tile([P, PACK, S], BF16, name="z2_rows")
-        scores, sent = [], []
-        for t in range(PACK):
-            both = keep.tile([P, 2 * S], F32, name=f"scores{t}")
-            nc.scalar.activation(both[:, S:], score_bank[t][:], ACT.Relu, scale=SIXTEENTH)
-            nc.scalar.activation(both[:, :S], score_bank[t][:], ACT.Copy, scale=gb_score[:, t : t + 1])
-            scores.append(both)
-            sent.append(keep.tile([P, 2 * S], F32, name=f"sent{t}"))
+        scores = [keep.tile([P, 2 * S], F32, name=f"scores{t}") for t in range(PACK)]
+        for n, (t, cols, entries) in enumerate(pieces):
+            nc.scalar.activation(scores[t][:, S + cols.start : S + cols.stop], score_bank[n][:], ACT.Relu, scale=SIXTEENTH)
+        for n, (t, cols, entries) in enumerate(pieces):
+            nc.scalar.activation(scores[t][:, cols], score_bank[n][:], ACT.Copy, scale=gb_score[:, t : t + 1])
 
-        half = S // 2
         tab_picked = keep.tile([P, PACK, S], F32, name="tab_picked")
         for t in range(PACK):
             for h in range(2):
-                nc.scalar.activation(
-                    tab_picked[:, t, h * half : (h + 1) * half], tab_t[t][:].indirect(n2_t[:, 16 * h : 16 * h + 16]), ACT.Copy
-                )
+                nc.scalar.activation(tab_picked[:, t, halves[h]], tab_t[t][:].indirect(n2_t[:, list_halves[h]]), ACT.Copy)
 
-        def send(t):
-            nc.vector.tensor_tensor(sent[t][:].indirect(n1_t[:]), scores[t][:, S:], ga_rows[:, t, :], ALU.mult)
+        sent = {}
 
-        def make_z(t):
-            nc.vector.scalar_tensor_tensor(z_rows[:, t, :], score_bank[t][:], ga_score[:, t : t + 1], sent[t][:, :S], ALU.mult, ALU.add)
+        def send(n):
+            t, cols, entries = pieces[n]
+            if t not in sent:
+                sent[t] = keep.tile([P, 2 * S], F32, name=f"sent{t}", tag="last" if t == PACK - 1 else f"sent{t}")
+            nc.vector.tensor_tensor(
+                sent[t][:].indirect(n1_t[:, entries]), scores[t][:, S + cols.start : S + cols.stop], ga_rows[:, t, cols], ALU.mult
+            )
+
+        def make_z(n, cols):
+            t, bank_cols, entries = pieces[n]
+            nc.vector.scalar_tensor_tensor(
+                z_rows[:, t, cols], score_bank[n][:, cols.start - bank_cols.start : cols.stop - bank_cols.start],
+                ga_score[:, t : t + 1], sent[t][:, cols], ALU.mult, ALU.add,
+            )
+
+        fetched = keep.tile([P, PACK, S], BF16, name="fetched", tag="last")
+        summed = keep.tile([P, PACK, S], BF16, name="summed")
 
         def make_z2(t):
-            fetched = keep.tile([P, S], F32, name=f"fetched{t}")
-            nc.scalar.activation(fetched[:], scores[t][:].indirect(n3_t[:]), ACT.Copy)
-            summed = keep.tile([P, S], F32, name=f"summed{t}")
-            nc.vector.scalar_tensor_tensor(summed[:], tab_picked[:, t, :], gb_abs[:, t : t + 1], scores[t][:, :S], ALU.mult, ALU.add)
-            nc.vector.tensor_tensor(z2_rows[:, t, :], summed[:], fetched[:], ALU.max)
+            nc.scalar.activation(fetched[:, t, :], scores[t][:].indirect(n3_t[:]), ACT.Copy)
+            nc.vector.scalar_tensor_tensor(summed[:, t, :], tab_picked[:, t, :], gb_abs[:, t : t + 1], scores[t][:, :S], ALU.mult, ALU.add)
 
         def interleave(copy, grouped, rows, cols):
             copy(
@@ -152,20 +160,18 @@ def tile_picked_simksendkindkdif_none_p_kernel(
                 rows[:, :, cols].rearrange("p t (c i) -> p c t i", i=4),
             )
 
-        send(0)
-        send(1)
-        make_z2(0)
-        make_z2(1)
-        make_z(0)
-        send(2)
-        make_z2(2)
-        make_z2(3)
-        make_z(1)
+        for n in range(len(pieces) - 1):
+            send(n)
+        for n in range(len(pieces) - 1):
+            make_z(n, pieces[n][1])
+        for t in range(PACK):
+            make_z2(t)
+        nc.vector.tensor_tensor(z2_rows[:], summed[:], fetched[:], ALU.max)
         z2_grouped = keep.tile([P, S, PACK], BF16, name="z2_grouped", align_bytes=64)
         interleave(nc.scalar.copy, z2_grouped, z2_rows, slice(0, S))
-        send(3)
-        make_z(2)
-        make_z(3)
+        send(len(pieces) - 1)
+        make_z(len(pieces) - 1, slice(0, P))
+        make_z(len(pieces) - 1, slice(P, S))
         z2_codes = keep.tile([P, S], U32, name="z2_codes", align_bytes=64)
         z2_plane = keep.tile([P, S], U8, name="z2_plane", align_bytes=64)
         nc.vector.quantize_mx(out=z2_codes[:].bitcast(FP8X4), scales=z2_plane[:], in_=z2_grouped[:].rearrange("p c t -> p (c t)"))
@@ -176,31 +182,32 @@ def tile_picked_simksendkindkdif_none_p_kernel(
         cm_bank = []
         for b in range(S // P):
             cols = slice(P * b, P * b + P)
-            interleave(nc.scalar.copy if b % 2 else nc.vector.tensor_copy, z_grouped, z_rows, cols)
+            interleave(nc.scalar.copy if b < 3 else nc.vector.tensor_copy, z_grouped, z_rows, cols)
         for b in range(S // P):
             cols = slice(P * b, P * b + P)
-            nc.vector.quantize_mx(out=z_codes[:, cols].bitcast(FP8X4), scales=z_plane[:, cols], in_=z_grouped[:, cols, :].rearrange("p c t -> p (c t)"))
-            bank = psum.tile([P, S], F32, name=f"cm_bank{b}")
+            plane = z2_plane[4:P, cols] if b == 0 else z_plane[:, cols]
+            nc.vector.quantize_mx(out=z_codes[:, cols].bitcast(FP8X4), scales=plane, in_=z_grouped[:, cols, :].rearrange("p c t -> p (c t)"))
+            bank = psum.tile([P, S], F32, name=f"cm_bank{b}", tag=f"bank{(5 + b) % 8}")
             nc.tensor.matmul_mx(
-                out=bank[:], lhsT=z_codes[:, cols].bitcast(FP8X4), lhsT_scale=z_plane[:, cols],
+                out=bank[:], lhsT=z_codes[:, cols].bitcast(FP8X4), lhsT_scale=plane,
                 rhs=z2_codes[:].bitcast(FP8X4), rhs_scale=z2_plane[:], start=True, stop=True,
             )
             cm_bank.append(bank)
 
-        for b in range(S // P):
-            cm = keep.tile([P, S], F32, name=f"cm{b}")
-            pulled = keep.tile([P, W], F32, name=f"pulled{b}")
-            second = keep.tile([P, W], F32, name=f"second{b}")
-            if b % 2 == 0:
-                nc.scalar.activation(cm[:], cm_bank[b][:], ACT.Copy, scale=SIXTEENTH)
-                nc.scalar.activation(pulled[:], cm[:].indirect(n5_t[:]), ACT.Copy, scale=-0.5)
-                nc.scalar.activation(second[:], cm[:].indirect(n4_t[:]), ACT.Copy)
-                for h in range(2):
-                    cols = slice(h * W // 2, (h + 1) * W // 2)
-                    nc.vector.tensor_tensor(cm[:].indirect(n4_t[:, 12 * h : 12 * h + 12]), second[:, cols], pulled[:, cols], ALU.add)
-            else:
-                nc.vector.tensor_scalar(cm[:], cm_bank[b][:], SIXTEENTH, None, ALU.mult)
-                nc.vector.tensor_tensor(pulled[:], cm[:].indirect(n5_t[:]), minus_half[:], ALU.mult)
-                nc.vector.tensor_tensor(second[:], cm[:].indirect(n4_t[:]), pulled[:], ALU.add)
-                nc.scalar.activation(cm[:].indirect(n4_t[:]), second[:], ACT.Copy)
-            nc.sync.dma_start(out[P * b : P * b + P, :], cm[:])
+        for pair in range(2):
+            even, odd = 2 * pair, 2 * pair + 1
+            cm = [keep.tile([P, S], F32, name=f"cm{b}") for b in (even, odd)]
+            pulled = [keep.tile([P, W], F32, name=f"pulled{b}") for b in (even, odd)]
+            second = [keep.tile([P, W], F32, name=f"second{b}") for b in (even, odd)]
+            nc.scalar.activation(cm[0][:], cm_bank[even][:], ACT.Copy, scale=SIXTEENTH)
+            nc.scalar.activation(pulled[0][:], cm[0][:].indirect(n5_t[:]), ACT.Copy, scale=-0.5)
+            nc.scalar.activation(second[0][:], cm[0][:].indirect(n4_t[:]), ACT.Copy)
+            nc.vector.tensor_scalar(cm[1][:], cm_bank[odd][:], SIXTEENTH, None, ALU.mult)
+            nc.vector.tensor_tensor(pulled[1][:], cm[1][:].indirect(n5_t[:]), minus_half[:], ALU.mult)
+            nc.vector.tensor_tensor(second[1][:], cm[1][:].indirect(n4_t[:]), pulled[1][:], ALU.add)
+            nc.scalar.activation(cm[1][:].indirect(n4_t[:]), second[1][:], ACT.Copy)
+            for h in range(2):
+                cols = slice(h * W // 2, (h + 1) * W // 2)
+                nc.vector.tensor_tensor(cm[0][:].indirect(n4_t[:, 12 * h : 12 * h + 12]), second[0][:, cols], pulled[0][:, cols], ALU.add)
+            for i, b in enumerate((even, odd)):
+                nc.sync.dma_start(out[P * b : P * b + P, :], cm[i][:])

@@ -39,20 +39,20 @@ def tile_picked_simksendkindkdif_none_p_kernel(
         planes = keep.tile([P, 2 * S], U8, name="planes", align_bytes=64)
         nc.gpsimd.memset(planes[:].bitcast(I32), 0)
 
-        ga_t = keep.tile([P, PACK], F32, name="ga_t")
-        gb_t = keep.tile([P, PACK], F32, name="gb_t")
         kidx_t = load_list("kidx_t", kidx)
-        nc.scalar.dma_start(gb_t[:], gb.rearrange("(p t) o -> p (t o)", t=PACK))
-        nc.scalar.dma_start(ga_t[:], ga.rearrange("(p t) o -> p (t o)", t=PACK))
         nc.sync.dma_start(d_scale_table[:].bitcast(I32), d_scales[0].bitcast(I32).unsqueeze(1).to_broadcast([16, 8, T // 4]))
         offs_t = load_list("offs_t", offs)
         nc.sync.dma_start(x_scale_table[:].bitcast(I32), x_scales[0].bitcast(I32).unsqueeze(1).to_broadcast([16, 8, T // 4]))
+        ga_t = keep.tile([P, PACK], F32, name="ga_t")
+        gb_t = keep.tile([P, PACK], F32, name="gb_t")
+        nc.sync.dma_start(gb_t[:], gb.rearrange("(p t) o -> p (t o)", t=PACK))
+        nc.sync.dma_start(ga_t[:], ga.rearrange("(p t) o -> p (t o)", t=PACK))
+        n2_t = load_list("n2_t", n2)
         d_word_table = keep.tile([P, T], I32, name="d_word_table", tag="table0")
         nc.sync.dma_start(d_word_table[:], d_words[0].rearrange("p n t -> p (n t)").bitcast(I32))
+        n1_t = load_list("n1_t", n1)
         x_word_table = keep.tile([P, T], I32, name="x_word_table", tag="table2")
         nc.sync.dma_start(x_word_table[:], x_words[0].rearrange("p n t -> p (n t)").bitcast(I32))
-        n2_t = load_list("n2_t", n2)
-        n1_t = load_list("n1_t", n1)
         n3_t = load_list("n3_t", n3)
         n4_t = load_list("n4_t", n4)
         n5_t = load_list("n5_t", n5)
@@ -156,7 +156,7 @@ def tile_picked_simksendkindkdif_none_p_kernel(
 
         def interleave(copy, grouped, rows, cols):
             copy(
-                grouped[:, cols, :].rearrange("p (c i) t -> p c t i", i=4),
+                grouped[:].rearrange("p (c i) t -> p c t i", i=4),
                 rows[:, :, cols].rearrange("p t (c i) -> p c t i", i=4),
             )
 
@@ -170,23 +170,20 @@ def tile_picked_simksendkindkdif_none_p_kernel(
         z2_grouped = keep.tile([P, S, PACK], BF16, name="z2_grouped", align_bytes=64)
         interleave(nc.scalar.copy, z2_grouped, z2_rows, slice(0, S))
         send(len(pieces) - 1)
-        make_z(len(pieces) - 1, slice(0, P))
-        make_z(len(pieces) - 1, slice(P, S))
+        make_z(len(pieces) - 1, slice(0, S))
         z2_codes = keep.tile([P, S], U32, name="z2_codes", align_bytes=64)
         z2_plane = keep.tile([P, S], U8, name="z2_plane", align_bytes=64)
         nc.vector.quantize_mx(out=z2_codes[:].bitcast(FP8X4), scales=z2_plane[:], in_=z2_grouped[:].rearrange("p c t -> p (c t)"))
 
-        z_grouped = keep.tile([P, S, PACK], BF16, name="z_grouped", align_bytes=64)
         z_codes = keep.tile([P, S], U32, name="z_codes", align_bytes=64)
         z_plane = keep.tile([P, S], U8, name="z_plane", align_bytes=64)
         cm_bank = []
         for b in range(S // P):
             cols = slice(P * b, P * b + P)
+            z_grouped = keep.tile([P, P, PACK], BF16, name=f"z_grouped{b}", tag=f"z_grouped{b % 3}", align_bytes=64)
             interleave(nc.scalar.copy if b < 3 else nc.vector.tensor_copy, z_grouped, z_rows, cols)
-        for b in range(S // P):
-            cols = slice(P * b, P * b + P)
             plane = z2_plane[4:P, cols] if b == 0 else z_plane[:, cols]
-            nc.vector.quantize_mx(out=z_codes[:, cols].bitcast(FP8X4), scales=plane, in_=z_grouped[:, cols, :].rearrange("p c t -> p (c t)"))
+            nc.vector.quantize_mx(out=z_codes[:, cols].bitcast(FP8X4), scales=plane, in_=z_grouped[:].rearrange("p c t -> p (c t)"))
             bank = psum.tile([P, S], F32, name=f"cm_bank{b}", tag=f"bank{(5 + b) % 8}")
             nc.tensor.matmul_mx(
                 out=bank[:], lhsT=z_codes[:, cols].bitcast(FP8X4), lhsT_scale=plane,
@@ -194,20 +191,33 @@ def tile_picked_simksendkindkdif_none_p_kernel(
             )
             cm_bank.append(bank)
 
-        for pair in range(2):
-            even, odd = 2 * pair, 2 * pair + 1
-            cm = [keep.tile([P, S], F32, name=f"cm{b}") for b in (even, odd)]
-            pulled = [keep.tile([P, W], F32, name=f"pulled{b}") for b in (even, odd)]
-            second = [keep.tile([P, W], F32, name=f"second{b}") for b in (even, odd)]
-            nc.scalar.activation(cm[0][:], cm_bank[even][:], ACT.Copy, scale=SIXTEENTH)
-            nc.scalar.activation(pulled[0][:], cm[0][:].indirect(n5_t[:]), ACT.Copy, scale=-0.5)
-            nc.scalar.activation(second[0][:], cm[0][:].indirect(n4_t[:]), ACT.Copy)
-            nc.vector.tensor_scalar(cm[1][:], cm_bank[odd][:], SIXTEENTH, None, ALU.mult)
-            nc.vector.tensor_tensor(pulled[1][:], cm[1][:].indirect(n5_t[:]), minus_half[:], ALU.mult)
-            nc.vector.tensor_tensor(second[1][:], cm[1][:].indirect(n4_t[:]), pulled[1][:], ALU.add)
-            nc.scalar.activation(cm[1][:].indirect(n4_t[:]), second[1][:], ACT.Copy)
-            for h in range(2):
-                cols = slice(h * W // 2, (h + 1) * W // 2)
-                nc.vector.tensor_tensor(cm[0][:].indirect(n4_t[:, 12 * h : 12 * h + 12]), second[0][:, cols], pulled[0][:, cols], ALU.add)
-            for i, b in enumerate((even, odd)):
-                nc.sync.dma_start(out[P * b : P * b + P, :], cm[i][:])
+        cm = [keep.tile([P, S if b % 2 else 2 * W], F32, name=f"cm{b}") for b in range(S // P)]
+        for b in (0, 2):
+            nc.gpsimd.memset(cm[b][:, S:], 0.0)
+        pulled = [keep.tile([P, W], F32, name=f"pulled{b}") for b in range(S // P)]
+        second = [keep.tile([P, W], F32, name=f"second{b}") for b in range(S // P)]
+
+        def fetch_on_scalar(b):
+            nc.scalar.activation(pulled[b][:], cm[b][:].indirect(n5_t[:]), ACT.Copy, scale=-0.5)
+            nc.scalar.activation(second[b][:], cm[b][:].indirect(n4_t[:]), ACT.Copy)
+
+        def put_on_vector(b):
+            nc.vector.tensor_tensor(cm[b][:].indirect(n4_t[:]), second[b][:], pulled[b][:], ALU.add)
+            nc.sync.dma_start(out[P * b : P * b + P, :], cm[b][:, :S])
+
+        def put_on_scalar(b):
+            nc.scalar.activation(cm[b][:].indirect(n4_t[:]), second[b][:], ACT.Copy)
+            nc.sync.dma_start(out[P * b : P * b + P, :], cm[b][:])
+
+        for b in (0, 2):
+            nc.scalar.activation(cm[b][:, :S], cm_bank[b][:], ACT.Copy, scale=SIXTEENTH)
+            fetch_on_scalar(b)
+        for b in (1, 3):
+            nc.vector.tensor_scalar(cm[b][:], cm_bank[b][:], SIXTEENTH, None, ALU.mult)
+        for b in (1, 3):
+            nc.vector.tensor_tensor(pulled[b][:], cm[b][:].indirect(n5_t[:]), minus_half[:], ALU.mult)
+        for b in (1, 3):
+            nc.vector.tensor_tensor(second[b][:], cm[b][:].indirect(n4_t[:]), pulled[b][:], ALU.add)
+        for b in (0, 2):
+            put_on_vector(b)
+            put_on_scalar(b + 1)

from contextlib import ExitStack

import concourse.mybir as mybir

K, T, S, W = 512, 2048, 512, 384
FLOPS = 2 * 2 * K * S * S

F32 = mybir.dt.float32
BF16 = mybir.dt.bfloat16
I32 = mybir.dt.int32
U32 = mybir.dt.uint32
U16 = mybir.dt.uint16
U8 = mybir.dt.uint8
FP8X4 = mybir.dt.float8_e4m3fn_x4
ALU = mybir.AluOpType
ACT = mybir.ActivationFunctionType

P = 128
PACK = 4
SIXTEENTH = 0.0625


def tile_picked_simksendkindkdif_none_p_kernel(
    tc, x_words, x_scales, d_words, d_scales, tab, ga, gb, offs, kidx, n1, n2, n3, n4, n5, out
):
    nc = tc.nc
    with ExitStack() as ctx:
        lists = ctx.enter_context(tc.tile_pool(name="lists", bufs=1))
        keep = ctx.enter_context(tc.tile_pool(name="keep", bufs=1))
        psum = ctx.enter_context(tc.psum_pool(name="psum", bufs=1))

        def load_list(name, src):
            tile = lists.tile(list(src.shape), U16, name=name)
            nc.sync.dma_start(tile[:], src)
            return tile

        d_scale_table = keep.tile([P, T], U8, name="d_scale_table")
        x_scale_table = keep.tile([P, T], U8, name="x_scale_table")
        planes = keep.tile([P, 2 * S], U8, name="planes", align_bytes=64)
        nc.gpsimd.memset(planes[:].bitcast(I32), 0)

        kidx_t = load_list("kidx_t", kidx)
        nc.sync.dma_start(d_scale_table[:].bitcast(I32), d_scales[0].bitcast(I32).unsqueeze(1).to_broadcast([16, 8, T // 4]))
        offs_t = load_list("offs_t", offs)
        nc.sync.dma_start(x_scale_table[:].bitcast(I32), x_scales[0].bitcast(I32).unsqueeze(1).to_broadcast([16, 8, T // 4]))
        ga_t = keep.tile([P, PACK], F32, name="ga_t")
        gb_t = keep.tile([P, PACK], F32, name="gb_t")
        nc.sync.dma_start(gb_t[:], gb.rearrange("(p t) o -> p (t o)", t=PACK))
        nc.sync.dma_start(ga_t[:], ga.rearrange("(p t) o -> p (t o)", t=PACK))
        n2_t = load_list("n2_t", n2)
        d_word_table = keep.tile([P, T], I32, name="d_word_table", tag="table0")
        nc.sync.dma_start(d_word_table[:], d_words[0].rearrange("p n t -> p (n t)").bitcast(I32))
        n1_t = load_list("n1_t", n1)
        x_word_table = keep.tile([P, T], I32, name="x_word_table", tag="table2")
        nc.sync.dma_start(x_word_table[:], x_words[0].rearrange("p n t -> p (n t)").bitcast(I32))
        n3_t = load_list("n3_t", n3)
        n4_t = load_list("n4_t", n4)
        n5_t = load_list("n5_t", n5)

        half_sign = keep.tile([P, PACK], F32, name="half_sign")
        gb_abs = keep.tile([P, PACK], F32, name="gb_abs")
        gb_score = keep.tile([P, PACK], F32, name="gb_score")
        ga_half = keep.tile([P, PACK], F32, name="ga_half")
        ga_score = keep.tile([P, PACK], F32, name="ga_score")
        nc.gpsimd.tensor_scalar(half_sign[:], gb_t[:], 0.0, 0.5, ALU.is_ge, ALU.subtract)
        nc.gpsimd.tensor_tensor(ga_half[:], ga_t[:], half_sign[:], ALU.mult)
        nc.gpsimd.tensor_scalar(ga_score[:], ga_half[:], -SIXTEENTH, 0.0, ALU.mult, ALU.add)
        nc.scalar.activation(gb_abs[:], gb_t[:], ACT.Abs)
        nc.scalar.activation(gb_score[:], gb_t[:], ACT.Abs, scale=SIXTEENTH)
        ga_rows = keep.tile([P, PACK, S], F32, name="ga_rows")
        nc.scalar.activation(ga_rows[:], ga_half[:].unsqueeze(2).to_broadcast([P, PACK, S]), ACT.Copy, scale=2.0)
        minus_half = keep.tile([P, W], F32, name="minus_half")
        nc.gpsimd.memset(minus_half[:], -0.5)

        d_bytes = keep.tile([P, S], U8, name="d_bytes")
        nc.vector.tensor_copy(d_bytes[:], d_scale_table[:].indirect(kidx_t[:]))
        staged = keep.tile([P, 2 * S], U8, name="staged", tag="table3")
        nc.vector.tensor_copy(
            staged[:, :S].rearrange("p (t m) -> p t m", t=PACK), d_bytes[:].rearrange("p (m t) -> p t m", t=PACK)
        )
        x_bytes = keep.tile([P, S], U8, name="x_bytes")
        nc.vector.tensor_copy(x_bytes[:], x_scale_table[:].indirect(offs_t[:]))
        nc.vector.tensor_copy(staged[:, S:].bitcast(I32), x_bytes[:].bitcast(I32))
        for q in range(4):
            nc.scalar.dma_start(planes[32 * q : 32 * q + 4, :].bitcast(I32), staged[32 * q : 32 * q + 32 : 8, :].bitcast(I32))

        d_picked = keep.tile([P, S], U32, name="d_picked", tag="table1")
        nc.vector.tensor_copy(d_picked[:], d_word_table[:].bitcast(U32).indirect(kidx_t[:]))
        d_codes = keep.tile([P, S], U32, name="d_codes", align_bytes=64)
        nc.vector.tensor_copy(
            d_codes[:].bitcast(I32).rearrange("p (t c i) -> p c t i", t=PACK, i=4),
            d_picked[:].bitcast(I32).rearrange("p (c i t) -> p c t i", t=PACK, i=4),
        )
        x_codes = keep.tile([P, S], U32, name="x_codes", align_bytes=64)
        half = S // 2
        halves = [slice(0, half), slice(half, S)]
        list_halves = [slice(0, half // 16), slice(half // 16, S // 16)]
        for h in range(2):
            nc.vector.tensor_copy(x_codes[:, halves[h]], x_word_table[:].bitcast(U32).indirect(offs_t[:, list_halves[h]]))

        tab_rows = tab.rearrange("(p t) j -> t p j", t=PACK)
        tab_t = []
        for t in range(PACK):
            tile = keep.tile([P, S], F32, name=f"tab{t}", tag=f"table{t}")
            nc.sync.dma_start(tile[:], tab_rows[t])
            tab_t.append(tile)

        pieces = [(0, halves[0], list_halves[0]), (0, halves[1], list_halves[1])]
        pieces = pieces + [(t, slice(0, S), slice(0, S // 16)) for t in range(1, PACK)]
        score_bank = []
        for n, (t, cols, entries) in enumerate(pieces):
            bank = psum.tile([P, cols.stop - cols.start], F32, name=f"score_bank{n}", tag=f"bank{n}")
            keys = slice(P * t, P * t + P)
            nc.tensor.matmul_mx(
                out=bank[:], lhsT=d_codes[:, keys].bitcast(FP8X4), lhsT_scale=planes[:, keys],
                rhs=x_codes[:, cols].bitcast(FP8X4), rhs_scale=planes[:, S + cols.start : S + cols.stop], start=True, stop=True,
            )
            score_bank.append(bank)

        z_rows = keep.tile([P, PACK, S], BF16, name="z_rows")
        z2_rows = keep.tile([P, PACK, S], BF16, name="z2_rows")
        scores = [keep.tile([P, 2 * S], F32, name=f"scores{t}") for t in range(PACK)]
        for n, (t, cols, entries) in enumerate(pieces):
            nc.scalar.activation(scores[t][:, S + cols.start : S + cols.stop], score_bank[n][:], ACT.Relu, scale=SIXTEENTH)
        for n, (t, cols, entries) in enumerate(pieces):
            nc.scalar.activation(scores[t][:, cols], score_bank[n][:], ACT.Copy, scale=gb_score[:, t : t + 1])

        tab_picked = keep.tile([P, PACK, S], F32, name="tab_picked")
        for t in range(PACK):
            for h in range(2):
                nc.scalar.activation(tab_picked[:, t, halves[h]], tab_t[t][:].indirect(n2_t[:, list_halves[h]]), ACT.Copy)

        sent = {}

        def send(n):
            t, cols, entries = pieces[n]
            if t not in sent:
                sent[t] = keep.tile([P, 2 * S], F32, name=f"sent{t}", tag="last" if t == PACK - 1 else f"sent{t}")
            nc.vector.tensor_tensor(
                sent[t][:].indirect(n1_t[:, entries]), scores[t][:, S + cols.start : S + cols.stop], ga_rows[:, t, cols], ALU.mult
            )

        def make_z(n, cols):
            t, bank_cols, entries = pieces[n]
            nc.vector.scalar_tensor_tensor(
                z_rows[:, t, cols], score_bank[n][:, cols.start - bank_cols.start : cols.stop - bank_cols.start],
                ga_score[:, t : t + 1], sent[t][:, cols], ALU.mult, ALU.add,
            )

        fetched = keep.tile([P, PACK, S], BF16, name="fetched", tag="last")
        summed = keep.tile([P, PACK, S], BF16, name="summed")

        def make_z2(t):
            nc.scalar.activation(fetched[:, t, :], scores[t][:].indirect(n3_t[:]), ACT.Copy)
            nc.vector.scalar_tensor_tensor(summed[:, t, :], tab_picked[:, t, :], gb_abs[:, t : t + 1], scores[t][:, :S], ALU.mult, ALU.add)

        def interleave(copy, grouped, rows, cols):
            copy(
                grouped[:].rearrange("p (c i) t -> p c t i", i=4),
                rows[:, :, cols].rearrange("p t (c i) -> p c t i", i=4),
            )

        for n in range(len(pieces) - 1):
            send(n)
        for n in range(len(pieces) - 1):
            make_z(n, pieces[n][1])
        for t in range(PACK):
            make_z2(t)
        nc.vector.tensor_tensor(z2_rows[:], summed[:], fetched[:], ALU.max)
        z2_grouped = keep.tile([P, S, PACK], BF16, name="z2_grouped", align_bytes=64)
        interleave(nc.scalar.copy, z2_grouped, z2_rows, slice(0, S))
        send(len(pieces) - 1)
        make_z(len(pieces) - 1, slice(0, S))
        z2_codes = keep.tile([P, S], U32, name="z2_codes", align_bytes=64)
        z2_plane = keep.tile([P, S], U8, name="z2_plane", align_bytes=64)
        nc.vector.quantize_mx(out=z2_codes[:].bitcast(FP8X4), scales=z2_plane[:], in_=z2_grouped[:].rearrange("p c t -> p (c t)"))

        z_codes = keep.tile([P, S], U32, name="z_codes", align_bytes=64)
        z_plane = keep.tile([P, S], U8, name="z_plane", align_bytes=64)
        cm_bank = []
        for b in range(S // P):
            cols = slice(P * b, P * b + P)
            z_grouped = keep.tile([P, P, PACK], BF16, name=f"z_grouped{b}", tag=f"z_grouped{b % 3}", align_bytes=64)
            interleave(nc.scalar.copy if b < 3 else nc.vector.tensor_copy, z_grouped, z_rows, cols)
            plane = z2_plane[4:P, cols] if b == 0 else z_plane[:, cols]
            nc.vector.quantize_mx(out=z_codes[:, cols].bitcast(FP8X4), scales=plane, in_=z_grouped[:].rearrange("p c t -> p (c t)"))
            bank = psum.tile([P, S], F32, name=f"cm_bank{b}", tag=f"bank{(5 + b) % 8}")
            nc.tensor.matmul_mx(
                out=bank[:], lhsT=z_codes[:, cols].bitcast(FP8X4), lhsT_scale=plane,
                rhs=z2_codes[:].bitcast(FP8X4), rhs_scale=z2_plane[:], start=True, stop=True,
            )
            cm_bank.append(bank)

        cm = [keep.tile([P, S if b % 2 else 2 * W], F32, name=f"cm{b}") for b in range(S // P)]
        for b in (0, 2):
            nc.gpsimd.memset(cm[b][:, S:], 0.0)
        pulled = [keep.tile([P, W], F32, name=f"pulled{b}") for b in range(S // P)]
        second = [keep.tile([P, W], F32, name=f"second{b}") for b in range(S // P)]

        def fetch_on_scalar(b):
            nc.scalar.activation(pulled[b][:], cm[b][:].indirect(n5_t[:]), ACT.Copy, scale=-0.5)
            nc.scalar.activation(second[b][:], cm[b][:].indirect(n4_t[:]), ACT.Copy)

        def put_on_vector(b):
            nc.vector.tensor_tensor(cm[b][:].indirect(n4_t[:]), second[b][:], pulled[b][:], ALU.add)
            nc.sync.dma_start(out[P * b : P * b + P, :], cm[b][:, :S])

        def put_on_scalar(b):
            nc.scalar.activation(cm[b][:].indirect(n4_t[:]), second[b][:], ACT.Copy)
            nc.sync.dma_start(out[P * b : P * b + P, :], cm[b][:])

        for b in (0, 2):
            nc.scalar.activation(cm[b][:, :S], cm_bank[b][:], ACT.Copy, scale=SIXTEENTH)
            fetch_on_scalar(b)
        for b in (1, 3):
            nc.vector.tensor_scalar(cm[b][:], cm_bank[b][:], SIXTEENTH, None, ALU.mult)
        for b in (1, 3):
            nc.vector.tensor_tensor(pulled[b][:], cm[b][:].indirect(n5_t[:]), minus_half[:], ALU.mult)
        for b in (1, 3):
            nc.vector.tensor_tensor(second[b][:], cm[b][:].indirect(n4_t[:]), pulled[b][:], ALU.add)
        for b in (0, 2):
            put_on_vector(b)
            put_on_scalar(b + 1)
